import numpy as np
import ml_dtypes


def mxq(x, axis, fmt="e4m3"):
    dtype, down = {"e4m3": (ml_dtypes.float8_e4m3fn, 7), "e5m2": (ml_dtypes.float8_e5m2, 14)}[fmt]
    v = np.moveaxis(np.asarray(x, np.float32).astype(ml_dtypes.bfloat16).astype(np.float64), axis, -1)
    blocks = v.reshape(v.shape[:-1] + (-1, 32))
    amax = np.abs(blocks).max(-1, keepdims=True)
    byte = np.maximum(np.where(amax > 0, np.frexp(amax)[1] - 1 + 127, 0) - down, 1)
    scale = np.exp2(byte - 127.0)
    codes = (blocks / scale).astype(np.float32).astype(dtype).astype(np.float64)
    return np.moveaxis((codes * scale).reshape(v.shape), -1, axis)


WIDE = False


def mx_kscale(k):
    if not WIDE:
        return np.ones(k)
    levels = np.array([10, -10, 5, -5, 0])
    if k % 512:
        return np.exp2(np.random.permutation(np.resize(levels, k // 32))).repeat(32)
    a = np.empty((k // 512, 16))
    for p in range(k // 512):
        a[p, :8] = np.random.permutation(np.resize(levels, 8))
        for g in range(8):
            far = levels[np.abs(levels - a[p, g]) >= 10]
            a[p, g + 8] = far[np.random.randint(len(far))]
    return np.exp2(a.ravel()).repeat(32)


BF16 = ml_dtypes.bfloat16


def bf(x):
    return np.asarray(x, np.float32).astype(BF16)


def f64(x):
    return np.asarray(x).astype(np.float64)

def planes(Y):
    n, m = Y.shape
    b = f64(bf(Y)).reshape(n // 32, 32, m)
    amax = np.abs(b).max(1)
    byte = np.clip(np.where(amax > 0, np.frexp(amax)[1] - 1 + 127 - 7, 1), 1, 254)
    codes = (b * np.exp2(127.0 - byte)[:, None, :]).reshape(n, m).astype(np.float32).astype(ml_dtypes.float8_e4m3fn).view(np.uint8)
    words = codes.reshape(n // 512, 128, 4, m).transpose(0, 1, 3, 2)
    return np.ascontiguousarray(words), np.ascontiguousarray(byte.astype(np.uint8).reshape(n // 512, 16, m))


M, D, F, P = 2048, 1024, 1536, 512


def setup_inputs():
    n = np.random.standard_normal
    sd, sp, t = mx_kscale(D), mx_kscale(P), mx_kscale(M)
    return {
        "x": bf(n((M, D)) * sd),
        "freq": bf(n((D, F)) / np.sqrt(D) / sd[:, None]),
        "phase": bf(np.random.uniform(-np.pi, np.pi, F)),
        "sample_weight": bf(M ** -0.25 * np.exp(0.3 * n(M)) * t),
        "coef": bf(M ** -0.25 * n((M, P)) * sp / t[:, None]),
        "mixing": bf(n((P, P)) / np.sqrt(P) / sp[:, None]),
        "amp": bf(np.exp(0.8 * n(F))),
        "out_scale": bf(np.exp(0.3 * n(P))),
    }


def reference(x, freq, phase, sample_weight, coef, mixing, amp, out_scale):
    z = mxq(f64(x), 1, "e4m3") @ mxq(f64(freq), 0, "e4m3")
    h = np.cos(z + f64(phase)) * f64(sample_weight)[:, None]
    c = mxq(f64(coef), 1, "e4m3") @ mxq(f64(mixing), 0, "e4m3")
    r = mxq(h, 0, "e4m3").T @ mxq(c, 0, "e4m3")
    y = r * f64(amp)[:, None] * f64(out_scale)
    Y = y
    words, scales = planes(Y)
    return y, words, scales

import math
from contextlib import ExitStack

import concourse.mybir as mybir
from concourse.masks import make_identity

M, D, F, P = 2048, 1024, 1536, 512
FLOPS = 2 * (M * D * F + M * P * P + F * M * P)

F32 = mybir.dt.float32
BF16 = mybir.dt.bfloat16
I32 = mybir.dt.int32
U32 = mybir.dt.uint32
U8 = mybir.dt.uint8
FP8X4 = mybir.dt.float8_e4m3fn_x4
ALU = mybir.AluOpType
ACT = mybir.ActivationFunctionType

TURN = 2.0 * math.pi
KB = 1024


def tile_mixed_fourier_primal_weights_h3_kernel(
    tc, x, freq, phase, sample_weight, coef, mixing, amp, out_scale, out_0, out_1, out_2
):
    nc = tc.nc
    with ExitStack() as ctx:
        raw = ctx.enter_context(tc.tile_pool(name="raw", bufs=1))
        keep = ctx.enter_context(tc.tile_pool(name="keep", bufs=1))
        psum = ctx.enter_context(tc.psum_pool(name="psum", bufs=1))
        ctx.enter_context(tc.manual_schedule())

        def sb(name, shape, dtype):
            return keep.tile(shape, dtype, name=name, align_bytes=64)

        def mx_pair(name, width=512):
            return (sb(name + "_codes", [128, width], U32), sb(name + "_scales", [128, width], U8))

        zbank = [psum.tile([128, 512], F32, name="zbank%d" % i) for i in range(4)]
        ring = [psum.tile([128, 512], F32, name="ring%d" % i) for i in range(4)]
        taken = []

        def take_bank():
            taken.append(0)
            return ring[(len(taken) - 1) % 4]

        stage = [sb("stage%d" % i, [128, 2048], BF16) for i in range(6)]
        hbuf = [sb("hbuf%d" % i, [128, 2048], BF16) for i in range(3)]
        x_mx = [[mx_pair("x%d%d" % (g, c)) for c in range(2)] for g in range(4)]
        f_mx = [[mx_pair("f%d%d" % (fc, c)) for c in range(2)] for fc in range(3)]
        coef_mx = [mx_pair("coef%d" % g) for g in range(4)]
        mix_mx = mx_pair("mix")
        c_mx = [mx_pair("c%d" % g) for g in range(4)]
        h_mx = [mx_pair("h%d" % i) for i in range(8)]
        y_codes = [sb("ycodes%d" % fc, [128, 512], U32) for fc in range(3)]
        y_scales = sb("yscales", [128, 3, 512], U8)
        turns = [sb("turns%d" % i, [128, 512], I32) for i in range(3)]
        rest = [sb("rest%d" % i, [128, 512], F32) for i in range(4)]
        cosz = [sb("cosz%d" % i, [128, 2048], F32) for i in range(2)]
        sw_all = sb("sw_all", [128, 4, 512], F32)
        ident = sb("ident", [128, 128], F32)
        vec_rows = sb("vec_rows", [128, 128], BF16)
        vec_f32 = sb("vec_f32", [128, 128], F32)
        sw_col = sb("sw_col", [128, 16], F32)
        shift = sb("shift", [128, 12], F32)
        shift_turns = sb("shift_turns", [128, 12], F32)
        amp_sb = sb("amp_sb", [128, 3, 4], BF16)
        oscale = sb("oscale", [128, 512], BF16)
        warm = sb("warm", [128, 1], F32)
        warm_out = sb("warm_out", [128, 1], F32)

        staged = {
            ("x", 0, 0): stage[0], ("f", 0, 0): stage[1], ("x", 0, 1): stage[2], ("f", 0, 1): stage[3],
            ("x", 1, 0): stage[4], ("x", 1, 1): stage[5], ("f", 1, 0): stage[5],
            ("x", 2, 0): stage[0], ("x", 2, 1): hbuf[0], ("mix",): stage[1],
            ("x", 3, 0): stage[2], ("x", 3, 1): hbuf[1], ("f", 1, 1): stage[3],
            ("coef", 0): stage[4], ("coef", 1): stage[0], ("coef", 2): stage[1], ("coef", 3): stage[2],
            ("c", 0): stage[5], ("f", 2, 0): stage[3], ("c", 1): stage[4], ("f", 2, 1): stage[0],
            ("c", 2): stage[1], ("c", 3): stage[2],
            ("y", 0): stage[3], ("y", 1): stage[4], ("y", 2): stage[5],
        }
        rawt = {}

        def load_x0(c):
            t = raw.tile([128, 4, 512], BF16, name="x0_%d" % c, offset=4 * KB * c)
            rawt["x", 0, c] = t
            nc.sync.dma_start(out=t[:], in_=x[0:512, 512 * c:512 * c + 512].rearrange("(p j) d -> p j d", j=4))

        def load_x(g):
            t = raw.tile([128, 4, 1024], BF16, name="x%d" % g, offset=8 * KB * g)
            rawt["x", g, 0] = t[:, :, 0:512]
            rawt["x", g, 1] = t[:, :, 512:1024]
            nc.sync.dma_start(out=t[:], in_=x[512 * g:512 * g + 512, :].rearrange("(p j) d -> p j d", j=4))

        def load_f(fc, c):
            t = raw.tile([128, 4, 512], BF16, name="f%d_%d" % (fc, c), offset=(32, 40, 0)[fc] * KB + 4 * KB * c)
            rawt["f", fc, c] = t
            src = freq[512 * c:512 * c + 512, 512 * fc:512 * fc + 512]
            nc.sync.dma_start(out=t[:], in_=src.rearrange("(p j) w -> p j w", j=4))

        def load_coef(g):
            t = raw.tile([128, 4, 512], BF16, name="coef%d" % g, offset=(48, 52, 8, 12)[g] * KB)
            rawt["coef", g] = t
            nc.sync.dma_start(out=t[:], in_=coef[512 * g:512 * g + 512, :].rearrange("(p j) d -> p j d", j=4))

        def load_mix():
            t = raw.tile([128, 4, 512], BF16, name="mixraw", offset=56 * KB)
            rawt["mix",] = t
            nc.sync.dma_start(out=t[:], in_=mixing.rearrange("(p j) w -> p j w", j=4))

        def quantize(src, pair):
            nc.vector.quantize_mx(out=pair[0][:].bitcast(FP8X4), scales=pair[1][:], in_=src[:])

        def q(*key):
            if key[0] == "x":
                quantize(staged[key], x_mx[key[1]][key[2]])
            elif key[0] == "f":
                quantize(staged[key], f_mx[key[1]][key[2]])
            elif key[0] == "coef":
                quantize(staged[key], coef_mx[key[1]])
            elif key[0] == "mix":
                quantize(staged[key], mix_mx)
            elif key[0] == "c":
                quantize(staged[key], c_mx[key[1]])
            elif key[0] == "h":
                quantize(hbuf[(key[1] + 2) % 3], h_mx[key[1] % 8])
            else:
                fc = key[1]
                nc.vector.quantize_mx(out=y_codes[fc][:].bitcast(FP8X4), scales=y_scales[:, fc, :], in_=staged[key][:])
                dst = out_1[fc].rearrange("p m t -> p (m t)").bitcast(I32)
                nc.sync.dma_start(out=dst, in_=y_codes[fc][:].bitcast(I32))

        def mm(out, lhs, lcols, rhs, rcols, start, stop):
            nc.tensor.matmul_mx(
                out=out, lhsT=lhs[0][:, lcols].bitcast(FP8X4), lhsT_scale=lhs[1][:, lcols],
                rhs=rhs[0][:, rcols].bitcast(FP8X4), rhs_scale=rhs[1][:, rcols], start=start, stop=stop)

        def copy_on(eng, out, in_):
            if eng == "S":
                nc.scalar.copy(out=out, in_=in_)
            elif eng == "V":
                nc.vector.tensor_copy(out=out, in_=in_)
            else:
                nc.gpsimd.tensor_scalar(out=out, in0=in_, scalar1=1.0, scalar2=0.0, op0=ALU.mult, op1=ALU.add)

        def x_turn(g, c, u):
            bank = take_bank()
            for e in range(2):
                words = rawt["x", g, c][:, 2 * u + e, :].bitcast(F32)
                for w in range(2):
                    a = 2 * e + w
                    nc.tensor.transpose(bank[:, 128 * a:128 * a + 128], words[:, w:256:2], ident[:])
            dst = staged["x", g, c][:].bitcast(F32)[:, 512 * u:512 * u + 512]
            nc.scalar.copy(out=dst.rearrange("k (p a) -> k p a", a=4), in_=bank[:].rearrange("k (a p) -> k p a", a=4))

        def coef_turn(g, h):
            bank = take_bank()
            for tt in range(2):
                words = rawt["coef", g][:, 2 * h + tt, :].bitcast(F32)
                for w in range(2):
                    a = 2 * tt + w
                    nc.tensor.transpose(bank[:, 128 * a:128 * a + 128], words[:, w:256:2], ident[:])
            dst = staged["coef", g][:].bitcast(F32)[:, 512 * h:512 * h + 512]
            nc.scalar.copy(out=dst.rearrange("k (t p w) -> k t p w", t=2, w=2),
                           in_=bank[:].rearrange("k (t w p) -> k t p w", t=2, w=2))

        def interleave(eng, key, src, lo, hi):
            dst = staged[key][:].rearrange("p (w j) -> p w j", j=4)[:, lo:hi, :]
            copy_on(eng, dst, src[:, :, lo:hi].rearrange("p j w -> p w j"))

        def il(key, half, eng="S"):
            interleave(eng, key, rawt[key], 256 * half, 256 * half + 256)

        held = {}

        def il_y(fc, half):
            interleave("S", ("y", fc), rawt["y", fc, 0], 256 * half, 256 * half + 256)

        def c_mm(g, n):
            bank = take_bank()
            held["c", g, n] = bank
            for t in range(4):
                mm(bank[:, 128 * t:128 * t + 128], coef_mx[g], slice(128 * t, 128 * t + 128),
                   mix_mx, slice(128 * n, 128 * n + 128), True, True)

        def c_out(g, n, eng):
            bank = held["c", g, n]
            dst = staged["c", g][:, 512 * n:512 * n + 512].rearrange("p (n t) -> p n t", t=4)
            copy_on(eng, dst, bank[:].rearrange("p (t n) -> p n t", t=4))

        def c_part(g, n):
            c_mm(g, n)
            c_out(g, n, "S")

        def sw_spread(g):
            bank = take_bank()
            held["sw", g] = bank
            for r in range(4):
                col = sw_col[:, 4 * g + r:4 * g + r + 1].to_broadcast([128, 128])
                nc.tensor.transpose(bank[:, 128 * r:128 * r + 128], col, ident[:])

        def sw_out(g):
            bank = held["sw", g]
            nc.vector.tensor_copy(out=sw_all[:, g, :].rearrange("q (u p e) -> q u p e", u=2, e=2),
                                  in_=bank[:].rearrange("q (p u e) -> q u p e", u=2, e=2))

        def z_tile(s, j):
            fc, g = divmod(s, 4)
            for c in range(2):
                mm(zbank[j][:], f_mx[fc][c], slice(128 * j, 128 * j + 128), x_mx[g][c], slice(0, 512), c == 0, c == 1)

        def whole_turns(s, j):
            col = 4 * (s // 4) + j
            nc.vector.tensor_scalar(out=turns[(4 * s + j) % 3][:], in0=zbank[j][:], scalar1=1.0 / TURN,
                                    scalar2=shift_turns[:, col:col + 1], op0=ALU.mult, op1=ALU.add)

        def remainder(s, j):
            col = 4 * (s // 4) + j
            nc.vector.scalar_tensor_tensor(out=rest[j][:], in0=zbank[j][:], scalar=1.0 / TURN,
                                           in1=turns[(4 * s + j) % 3][:], op0=ALU.mult, op1=ALU.subtract)
            nc.scalar.activation(out=cosz[s % 2][:, 512 * j:512 * j + 512], in_=rest[j][:], func=ACT.Sin,
                                 bias=shift[:, col:col + 1], scale=TURN)
            if s < 11:
                z_tile(s + 1, j)

        def weigh(eng, s, j0, n):
            cols = slice(512 * j0, 512 * (j0 + n))
            w = sw_all[:, s % 4:s % 4 + 1, :].to_broadcast([128, n, 512])
            eng.tensor_tensor(out=hbuf[s % 3][:, cols].rearrange("p (j m) -> p j m", j=n),
                              in0=cosz[s % 2][:, cols].rearrange("p (j m) -> p j m", j=n), in1=w, op=ALU.mult)

        def h_turn(s, h, eng="S"):
            bank = take_bank()
            words = hbuf[s % 3][:].bitcast(F32)
            for u in range(2):
                for jj in range(2):
                    lo = 256 * (2 * h + jj) + 128 * u
                    a = 2 * u + jj
                    nc.tensor.transpose(bank[:, 128 * a:128 * a + 128], words[:, lo:lo + 128], ident[:])
            dst = hbuf[(s + 2) % 3][:].bitcast(F32).rearrange("q (t m u) -> q t m u", t=4, u=2)
            copy_on(eng, dst[:, :, 64 * h:64 * h + 64, :], bank[:].rearrange("q (u m t) -> q t m u", u=2, t=4))

        def r_passes(bank, fc, t, groups):
            for g in groups:
                mm(bank[:], h_mx[(4 * fc + g) % 8], slice(128 * t, 128 * t + 128), c_mx[g], slice(0, 512), g == 0, g == 3)

        def y_rows(bank, fc, t, lo=0, hi=512):
            if t == 0:
                rawt["y", fc, lo] = raw.tile([128, 4, hi - lo], F32, name="y%d_%d" % (fc, lo),
                                             offset=(16, 24, 32)[fc] * KB + 16 * lo)
            yt = rawt["y", fc, lo]
            nc.vector.scalar_tensor_tensor(out=yt[:, t, :], in0=bank[:, lo:hi], scalar=amp_sb[:, fc, t:t + 1],
                                           in1=oscale[:, lo:hi], op0=ALU.mult, op1=ALU.mult)

        def y_store(fc, ts, lo, hi):
            dst = out_0[512 * fc:512 * fc + 512, :].rearrange("(p t) m -> p t m", t=4)
            nc.sync.dma_start(out=dst[:, ts, lo:hi], in_=rawt["y", fc, lo][:, ts, :])

        def r_mm(fc, t):
            held["r", fc, t] = take_bank()
            r_passes(held["r", fc, t], fc, t, range(4))

        def r_out(fc, t):
            y_rows(held["r", fc, t], fc, t)
            y_store(fc, slice(t, t + 1), 0, 512)

        load_x0(0)
        nc.vector.memset(vec_rows[:], 0.0)
        nc.vector.memset(warm[:], 0.0)
        nc.scalar.activation(out=warm_out[:], in_=warm[:], func=ACT.Sin)
        make_identity(nc, ident[:])
        load_x0(1)
        nc.sync.dma_start(out=vec_rows[0:12, :], in_=phase.rearrange("(r p) -> r p", p=128))
        nc.sync.dma_start(out=vec_rows[12:28, :], in_=sample_weight.rearrange("(r p) -> r p", p=128))
        load_f(0, 0)
        load_f(0, 1)
        load_x(1)
        load_x(2)
        load_f(1, 0)
        load_x(3)
        load_f(1, 1)
        load_mix()
        load_coef(0)
        load_coef(1)

        for c in range(2):
            for u in range(2):
                x_turn(0, c, u)
        nc.vector.tensor_copy(out=vec_f32[:], in_=vec_rows[:])
        vbank = take_bank()
        nc.tensor.transpose(vbank[:, 0:128], vec_f32[:], ident[:])
        q("x", 0, 0)
        interleave("V", ("f", 0, 0), rawt["f", 0, 0], 0, 384)
        interleave("S", ("f", 0, 0), rawt["f", 0, 0], 384, 512)
        nc.vector.tensor_scalar(out=shift[:], in0=vbank[:, 0:12], scalar1=1.0, scalar2=TURN / 4, op0=ALU.mult, op1=ALU.add)
        nc.vector.tensor_copy(out=sw_col[:], in_=vbank[:, 12:28])
        interleave("V", ("f", 0, 1), rawt["f", 0, 1], 0, 256)
        interleave("S", ("f", 0, 1), rawt["f", 0, 1], 256, 512)
        q("x", 0, 1)
        nc.vector.tensor_scalar(out=shift_turns[:], in0=shift[:], scalar1=1.0 / TURN, scalar2=0.0, op0=ALU.mult, op1=ALU.add)
        q("f", 0, 0)
        q("f", 0, 1)
        sw_spread(0)
        for j in range(4):
            z_tile(0, j)
        sw_out(0)
        for c in range(2):
            for u in range(2):
                x_turn(1, c, u)
        load_f(2, 0)
        load_f(2, 1)
        load_coef(2)
        load_coef(3)
        nc.sync.dma_start(out=amp_sb[:], in_=amp.rearrange("(c p t) -> p c t", p=128, t=4))
        nc.sync.dma_start(out=oscale[:], in_=out_scale.partition_broadcast(128))

        def job(fn, *args):
            return lambda: fn(*args)

        batches = {
            1: [("x", 2, 0), ("x", 2, 1)],
            2: [("f", 1, 0), ("x", 3, 0), ("x", 3, 1)],
            3: [("mix",), ("f", 1, 1)],
            4: [("coef", 0), ("coef", 1)],
            5: [("coef", 2), ("c", 0)],
            6: [("coef", 3), ("c", 1), ("f", 2, 0)],
            7: [("c", 2), ("f", 2, 1)],
            8: [("c", 3)],
            11: [("y", 0)],
        }
        side = {
            0: ([], [job(q, "x", 1, 0), job(q, "x", 1, 1), job(interleave, "G", ("f", 1, 0), rawt["f", 1, 0], 0, 512)],
                [job(x_turn, 2, 0, 0), job(x_turn, 2, 0, 1)], [job(x_turn, 2, 1, 0), job(x_turn, 2, 1, 1)],
                []),
            1: ([job(sw_spread, 1), job(x_turn, 3, 0, 0), job(x_turn, 3, 0, 1)], [job(sw_out, 1)], [job(x_turn, 3, 1, 0), job(x_turn, 3, 1, 1)], [],
                [job(il, ("f", 1, 1), 0)]),
            2: ([job(sw_spread, 2), job(il, ("f", 1, 1), 1)], [job(sw_out, 2)], [job(il, ("mix",), 0)], [job(il, ("mix",), 1)],
                []),
            3: ([job(sw_spread, 3), job(coef_turn, 0, 0), job(coef_turn, 0, 1)], [job(sw_out, 3)], [job(coef_turn, 1, 0), job(coef_turn, 1, 1)], [job(coef_turn, 2, 0), job(coef_turn, 2, 1)],
                []),
            4: ([job(il, ("f", 2, 0), 0), job(c_mm, 0, 3), job(c_part, 0, 0)], [], [job(c_out, 0, 3, "V"), job(c_part, 0, 1), job(c_part, 0, 2)], [],
                [job(il, ("f", 2, 0), 1)]),
            5: ([job(c_mm, 1, 3), job(c_part, 1, 0), job(c_part, 1, 1)], [], [job(c_out, 1, 3, "V"), job(c_part, 1, 2)], [job(coef_turn, 3, 0), job(coef_turn, 3, 1)],
                [job(il, ("f", 2, 1), 0)]),
            6: ([job(c_mm, 2, 3), job(c_part, 2, 0), job(c_part, 2, 1)], [], [job(c_out, 2, 3, "V"), job(c_part, 2, 2), job(il, ("f", 2, 1), 1)], [],
                []),
            7: ([job(c_mm, 3, 3), job(c_part, 3, 0), job(c_part, 3, 1)], [], [job(c_out, 3, 3, "V"), job(c_part, 3, 2)], [],
                []),
            8: ([job(r_mm, 0, 0), job(r_mm, 0, 1)], [], [job(r_out, 0, 0)], [job(r_out, 0, 1)], []),
            9: ([job(r_mm, 0, 2), job(r_mm, 0, 3)], [], [job(r_out, 0, 2)], [job(r_out, 0, 3)], []),
            10: ([job(r_mm, 1, 0), job(r_mm, 1, 1), job(il_y, 0, 0)], [], [job(r_out, 1, 0), job(il_y, 0, 1)], [job(r_out, 1, 1)], []),
            11: ([job(r_mm, 1, 2), job(r_mm, 1, 3)], [job(r_out, 1, 2)], [job(r_out, 1, 3)], [job(il_y, 1, 0)], []),
        }

        def run(jobs):
            for jb in jobs:
                jb()

        for s in range(12):
            if s >= 2:
                h_turn(s - 2, 1)
            for key in batches.get(s, []):
                q(*key)
            if s >= 3:
                q("h", s - 3)
            if s >= 1:
                weigh(nc.gpsimd, s - 1, 0, 2)
                weigh(nc.gpsimd, s - 1, 2, 2)
            run(side[s][0])
            whole_turns(s, 0)
            whole_turns(s, 1)
            run(side[s][1])
            remainder(s, 0)
            run(side[s][2])
            whole_turns(s, 2)
            remainder(s, 1)
            if s >= 1:
                h_turn(s - 1, 0)
            run(side[s][3])
            whole_turns(s, 3)
            remainder(s, 2)
            remainder(s, 3)
            run(side[s][4])

        h_turn(10, 1)
        q("h", 9)
        for t in range(4):
            r_passes(zbank[t], 2, t, range(2))
        weigh(nc.vector, 11, 0, 1)
        weigh(nc.vector, 11, 1, 1)
        h_turn(11, 0)
        weigh(nc.vector, 11, 2, 1)
        weigh(nc.vector, 11, 3, 1)
        h_turn(11, 1)
        il_y(1, 1)
        q("h", 10)
        for t in range(4):
            r_passes(zbank[t], 2, t, range(2, 3))
        q("h", 11)
        for t in range(4):
            r_passes(zbank[t], 2, t, range(3, 4))
        q("y", 1)
        for n in range(4):
            lo, hi = 128 * n, 128 * n + 128
            for t in range(4):
                y_rows(zbank[t], 2, t, lo, hi)
            y_store(2, slice(0, 4), lo, hi)
            dst = staged["y", 2][:, 4 * lo:4 * hi].rearrange("p (w j) -> p w j", j=4)
            copy_on("S" if n < 3 else "V", dst, rawt["y", 2, lo][:].rearrange("p j w -> p w j"))
        q("y", 2)
        for quad in range(4):
            eng = nc.scalar if quad % 2 == 0 else nc.sync
            eng.dma_start(out=out_2[:, 4 * quad:4 * quad + 4, :].rearrange("g r m -> r g m").bitcast(I32),
                          in_=y_scales[32 * quad:32 * quad + 4, :, :].bitcast(I32))
